import numpy as np
import ml_dtypes


def mxq(x, axis, fmt="e4m3"):
    dtype, down = {"e4m3": (ml_dtypes.float8_e4m3fn, 7), "e5m2": (ml_dtypes.float8_e5m2, 14)}[fmt]
    v = np.moveaxis(np.asarray(x, np.float32).astype(ml_dtypes.bfloat16).astype(np.float64), axis, -1)
    blocks = v.reshape(v.shape[:-1] + (-1, 32))
    amax = np.abs(blocks).max(-1, keepdims=True)
    byte = np.maximum(np.where(amax > 0, np.frexp(amax)[1] - 1 + 127, 0) - down, 1)
    scale = np.exp2(byte - 127.0)
    codes = (blocks / scale).astype(np.float32).astype(dtype).astype(np.float64)
    return np.moveaxis((codes * scale).reshape(v.shape), -1, axis)


WIDE = False


def mx_kscale(k):
    if not WIDE:
        return np.ones(k)
    levels = np.array([10, -10, 5, -5, 0])
    if k % 512:
        return np.exp2(np.random.permutation(np.resize(levels, k // 32))).repeat(32)
    a = np.empty((k // 512, 16))
    for p in range(k // 512):
        a[p, :8] = np.random.permutation(np.resize(levels, 8))
        for g in range(8):
            far = levels[np.abs(levels - a[p, g]) >= 10]
            a[p, g + 8] = far[np.random.randint(len(far))]
    return np.exp2(a.ravel()).repeat(32)


def f64(x):
    return np.asarray(x).astype(np.float64)


def striped(idx):
    return np.tile(idx.reshape(-1, 16).T, (8, 1)).astype(np.uint16)


def unstriped(offs):
    return offs[:16].T.reshape(-1).astype(np.int64)


E2M1 = np.array([0.0, 0.5, 1.0, 1.5, 2.0, 3.0, 4.0, 6.0, -0.0, -0.5, -1.0, -1.5, -2.0, -3.0, -4.0, -6.0])


def pack_weight(w, fmt):
    k, n = w.shape
    w = f64(np.asarray(w, np.float32).astype(ml_dtypes.bfloat16)).reshape(k // 32, 32, n)
    amax = np.abs(w).max(1)
    if fmt == "e4m3":
        byte = np.frexp(amax)[1] - 1 + 127 - 7
    else:
        mant, ex = np.frexp(amax / 6.0)
        byte = np.where(mant > 0.5, ex, ex - 1) + 127
    byte = np.clip(np.where(amax > 0, byte, 1), 1, 254)
    scaled = (w * np.exp2(127.0 - byte)[:, None, :]).reshape(k, n).astype(np.float32)
    by_word = np.ascontiguousarray(scaled.reshape(k // 512, 128, 4, n).transpose(0, 1, 3, 2))
    if fmt == "e4m3":
        words = by_word.astype(ml_dtypes.float8_e4m3fn).view(np.uint8)
    else:
        c = by_word.astype(ml_dtypes.float4_e2m1fn).view(np.uint8) & 0xF
        words = (c[..., 0::2] | (c[..., 1::2] << 4)).reshape(k // 512, 128, 2 * n)
    return np.ascontiguousarray(words), np.ascontiguousarray(byte.astype(np.uint8).reshape(k // 512, 16, n))


def unpack_weight(words, scales, fmt):
    g, _, n = scales.shape
    words = np.ascontiguousarray(words).reshape(g, 128, n, -1)
    if fmt == "e4m3":
        vals = words.view(ml_dtypes.float8_e4m3fn).astype(np.float64)
    else:
        nib = np.empty((g, 128, n, 4), np.uint8)
        nib[..., 0::2] = words & 0xF
        nib[..., 1::2] = words >> 4
        vals = E2M1[nib]
    vals = vals * np.repeat(np.exp2(scales.astype(np.float64) - 127.0), 8, axis=1)[..., None]
    return vals.transpose(0, 1, 3, 2).reshape(g * 512, n)


def gelu(v):
    return 0.5 * v * (1.0 + np.tanh(np.sqrt(2.0 / np.pi) * (v + 0.044715 * v**3)))


K, H, T, S, T3, S2, T2 = 1024, 1024, 2048, 512, 2048, 512, 1024

def setup_inputs():
    n = np.random.standard_normal
    s = mx_kscale(K)[:, None]
    u = s
    tab_words, tab_scales = pack_weight(n((K, T)) * s, "e4m3")
    tab2_words, tab2_scales = pack_weight(n((H, T3)) / np.sqrt(H) / u, "e4m3")
    w4_words, w4_scales = pack_weight(1.6 * n((K, H)) / np.sqrt(K) / s, "e2m1")
    return {
        "tab_words": tab_words, "tab_scales": tab_scales,
        "offs": striped(np.random.permutation(T)[:S]),
        "tab2_words": tab2_words, "tab2_scales": tab2_scales,
        "offs2": striped(np.random.permutation(T3)[:S2]),
        "offs3": striped(np.random.permutation(T2)[:S]),
        "w1": (1.6 * n((K, H)) / np.sqrt(K) / s).astype(np.float32),
        "w4_words": w4_words, "w4_scales": w4_scales,
        "gain": (0.6 * np.exp(0.3 * n(H)) * u[:, 0]).astype(np.float32),
        "pv": n(S2).astype(np.float32),
        "page1": n((S2, T2)).astype(np.float32),
        "wgo": np.exp(0.3 * n((128, S))).astype(np.float32),
    }

def reference(tab_words, tab_scales, offs, tab2_words, tab2_scales, offs2, offs3, w1, w4_words, w4_scales, gain, pv, page1, wgo):
    v = unpack_weight(tab_words, tab_scales, "e4m3")[:, unstriped(offs)]
    v2 = unpack_weight(tab2_words, tab2_scales, "e4m3")[:, unstriped(offs2)]
    w4 = unpack_weight(w4_words, w4_scales, "e2m1")
    w1q = mxq(f64(w1), 0, "e4m3")
    a = w1q.T @ v
    b = w4.T @ v
    h = f64(gain)[:, None] * (np.maximum(a, b) + np.tanh(a))
    hq = mxq(h, 0, "e4m3")
    e = v2.T @ hq
    d = v2.T @ v
    score = e + np.tanh(d + f64(pv)[:, None])
    out = f64(page1).copy()
    out[:, unstriped(offs3)] = np.tile(f64(wgo), (S2 // 128, 1)) * score
    return out

@@ -1,0 +1,267 @@
+from contextlib import ExitStack
+
+import concourse.mybir as mybir
+from concourse.masks import make_identity
+
+K, H, T, S, S2, T2 = 1024, 1024, 2048, 512, 512, 1024
+FLOPS = 2 * (2 * K * H * S + H * S2 * S + K * S2 * S)
+
+F32 = mybir.dt.float32
+BF16 = mybir.dt.bfloat16
+I32 = mybir.dt.int32
+U32 = mybir.dt.uint32
+U16 = mybir.dt.uint16
+U8 = mybir.dt.uint8
+FP8X4 = mybir.dt.float8_e4m3fn_x4
+FP4X4 = mybir.dt.float4_e2m1fn_x4
+ALU = mybir.AluOpType
+ACT = mybir.ActivationFunctionType
+
+P = 128
+PACK = 4
+KP = P * PACK
+PASSES = K // KP
+RB = H // KP
+JB = S // P
+MB = S2 // P
+V2_ROW = 4
+CAST_COLS = 256
+CAST_ENGINES = "vvvsssss"
+GROUPS = 1
+
+
+def tile_list_attempt_page_scores_kernel(
+    tc, tab_words, tab_scales, offs, tab2_words, tab2_scales, offs2, offs3,
+    w1, w4_words, w4_scales, gain, pv, page1, wgo, out,
+):
+    nc = tc.nc
+    with ExitStack() as ctx:
+        keep = ctx.enter_context(tc.tile_pool(name="keep", bufs=1))
+        ring = ctx.enter_context(tc.tile_pool(name="ring", bufs=3))
+        psum_ab = ctx.enter_context(tc.psum_pool(name="psum_ab", bufs=3))
+        psum_x = ctx.enter_context(tc.psum_pool(name="psum_x", bufs=2))
+        psum_de = ctx.enter_context(tc.psum_pool(name="psum_de", bufs=3))
+
+        def kept(shape, dtype, name):
+            return keep.tile(shape, dtype, name=name, align_bytes=64)
+
+        list1 = kept([P, S // 16], U16, "list1")
+        list2 = kept([P, S2 // 16], U16, "list2")
+        list3 = kept([P, S // 16], U16, "list3")
+        tab_w = [kept([P, T], U32, f"tab_w{a}") for a in range(PASSES)]
+        tab2_w = [kept([P, T], U32, f"tab2_w{a}") for a in range(PASSES)]
+        tab_s = kept([P, PASSES * T], U8, "tab_s")
+        tab2_s = kept([P, T], U8, "tab2_s")
+        w4_w = kept([P, PASSES, 2 * H], U8, "w4_w")
+        w4_s = kept([P, PASSES * H], U8, "w4_s")
+        w1_raw = [[kept([P, PACK, KP], F32, f"w1_raw{rb}{a}") for a in range(PASSES)] for rb in range(RB)]
+        gain_sb = kept([P, RB, PACK], F32, "gain_sb")
+        pv_sb = kept([P, MB], F32, "pv_sb")
+        wgo_sb = kept([P, S], F32, "wgo_sb")
+        page = [kept([P, T2], F32, f"page{mb}") for mb in range(MB)]
+        ident = kept([P, P], F32, "ident")
+
+        rows = kept([P, KP], F32, "rows")
+        make_identity(nc, ident[:])
+        nc.gpsimd.memset(rows[:], 0.0)
+        nc.vector.memset(tab_s[:].bitcast(I32), 0)
+        nc.vector.memset(w4_s[:].bitcast(I32), 0)
+        nc.vector.memset(tab2_s[:].bitcast(I32), 0)
+
+        def load_words(tile, words):
+            nc.sync.dma_start(tile[:].bitcast(I32), words.rearrange("p t i -> p (t i)").bitcast(I32))
+
+        def load_planes(tile, scales):
+            for q in range(4):
+                nc.sync.dma_start(
+                    tile[32 * q : 32 * q + 4, :].bitcast(I32).rearrange("r (a c) -> r a c", a=PASSES),
+                    scales[:, 4 * q : 4 * q + 4, :].rearrange("a r c -> r a c").bitcast(I32),
+                )
+
+        nc.sync.dma_start(list1[:], offs)
+        nc.sync.dma_start(w4_w[:].bitcast(I32), w4_words.rearrange("a p c -> p a c").bitcast(I32))
+        load_planes(tab_s, tab_scales)
+        for a in range(PASSES):
+            load_words(tab_w[a], tab_words[a])
+        load_planes(w4_s, w4_scales)
+        nc.sync.dma_start(rows[0:RB, :], gain.rearrange("(b r) -> b r", b=RB))
+        nc.sync.dma_start(rows[RB : RB + 1, :], pv.rearrange("(o m) -> o m", o=1))
+        for rb in range(RB):
+            for a in range(PASSES):
+                nc.sync.dma_start(
+                    w1_raw[rb][a][:],
+                    w1[a * KP : (a + 1) * KP, rb * KP : (rb + 1) * KP].rearrange("(p j) c -> p j c", j=PACK),
+                )
+        nc.sync.dma_start(list2[:], offs2)
+        nc.sync.dma_start(list3[:], offs3)
+        for a in range(PASSES):
+            load_words(tab2_w[a], tab2_words[a])
+        nc.sync.dma_start(wgo_sb[:], wgo)
+        for mb in range(MB):
+            nc.sync.dma_start(page[mb][:], page1[mb * P : (mb + 1) * P, :])
+
+        for q in range(4):
+            nc.gpsimd.dma_start(
+                tab2_s[32 * q + V2_ROW : 32 * q + V2_ROW + 4 * PASSES, :].bitcast(I32),
+                tab2_scales[:, 4 * q : 4 * q + 4, :].bitcast(I32),
+            )
+        bank = psum_x.tile([P, PACK, P], F32, name="turned")
+        for t in range(PACK):
+            nc.tensor.transpose(bank[:, t, :], rows[:, t::PACK], ident[:])
+        nc.scalar.copy(gain_sb[:], bank[:, :, 0:RB].rearrange("p t b -> p b t"))
+        bank = psum_x.tile([P, PACK, P], F32, name="turned")
+        for mb in range(MB):
+            nc.tensor.transpose(bank[:, mb, :], rows[:, mb * P : (mb + 1) * P], ident[:])
+        nc.scalar.copy(pv_sb[:], bank[:, :, RB])
+
+        v_s = [kept([P, S], U8, f"v_s{a}") for a in range(PASSES)]
+        v_w = [kept([P, S], U32, f"v_w{a}") for a in range(PASSES)]
+        for a in range(PASSES):
+            nc.vector.tensor_copy(v_s[a][:], tab_s[:, a * T : (a + 1) * T].indirect(list1[:]))
+        for a in range(PASSES):
+            nc.vector.tensor_copy(v_w[a][:], tab_w[a][:].indirect(list1[:]))
+        v2_s = kept([P, S2], U8, "v2_s")
+        v2_w = [kept([P, S2], U32, f"v2_w{a}") for a in range(PASSES)]
+
+        def dealt(bank):
+            return bank[:].rearrange("p (m t) -> p t m", t=PACK)
+
+        b_sb = {}
+
+        def second_features(rb, jb):
+            js = slice(jb * P, (jb + 1) * P)
+            bank = psum_ab.tile([P, KP], F32, name="ab")
+            for a in range(PASSES):
+                nc.tensor.matmul_mx(
+                    out=bank[:],
+                    lhsT=v_w[a][:, js].bitcast(FP8X4), lhsT_scale=v_s[a][:, js],
+                    rhs=w4_w[:, a, 2 * rb * KP : 2 * (rb + 1) * KP].bitcast(FP4X4),
+                    rhs_scale=w4_s[:, a * H + rb * KP : a * H + (rb + 1) * KP],
+                    start=(a == 0), stop=(a == PASSES - 1),
+                )
+            b_sb[rb, jb] = kept([P, PACK, P], F32, f"b_sb{rb}{jb}")
+            nc.scalar.copy(b_sb[rb, jb][:], dealt(bank))
+
+        w1_w = [[kept([P, KP], U32, f"w1_w{rb}{a}") for a in range(PASSES)] for rb in range(RB)]
+        w1_s = [[kept([P, KP], U8, f"w1_s{rb}{a}") for a in range(PASSES)] for rb in range(RB)]
+        w1_bf = [[kept([P, KP, PACK], BF16, f"w1_bf{rb}{a}") for a in range(PASSES)] for rb in range(RB)]
+
+        def round_w1(rb, a):
+            for piece in range(KP // CAST_COLS):
+                cs = slice(piece * CAST_COLS, (piece + 1) * CAST_COLS)
+                dst = w1_bf[rb][a][:, cs, :].rearrange("p (c i) j -> p c j i", i=4)
+                src = w1_raw[rb][a][:, :, cs].rearrange("p j (c i) -> p c j i", i=4)
+                eng = CAST_ENGINES[(rb * PASSES + a) * (KP // CAST_COLS) + piece]
+                if eng == "v":
+                    nc.vector.tensor_copy(dst, src)
+                elif eng == "g":
+                    nc.gpsimd.tensor_copy(dst, src)
+                else:
+                    nc.scalar.copy(dst, src)
+
+        def quantize_w1(rb, a):
+            nc.vector.quantize_mx(
+                out=w1_w[rb][a][:].bitcast(FP8X4), scales=w1_s[rb][a][:],
+                in_=w1_bf[rb][a][:].rearrange("p c j -> p (c j)"),
+            )
+
+        h_bf = [kept([P, S, PACK], BF16, f"h_bf{rb}") for rb in range(RB)]
+        h_w = [kept([P, S], U32, f"h_w{rb}") for rb in range(RB)]
+        h_s = [kept([P, S], U8, f"h_s{rb}") for rb in range(RB)]
+        parts = {}
+
+        def first_features(rb, jb):
+            js = slice(jb * P, (jb + 1) * P)
+            bank = psum_ab.tile([P, KP], F32, name="ab")
+            for a in range(PASSES):
+                nc.tensor.matmul_mx(
+                    out=bank[:],
+                    lhsT=v_w[a][:, js].bitcast(FP8X4), lhsT_scale=v_s[a][:, js],
+                    rhs=w1_w[rb][a][:].bitcast(FP8X4), rhs_scale=w1_s[rb][a][:],
+                    start=(a == 0), stop=(a == PASSES - 1),
+                )
+            larger = ring.tile([P, PACK, P], F32, name="larger")
+            bent = ring.tile([P, PACK, P], F32, name="bent")
+            nc.scalar.activation(bent[:], dealt(bank), ACT.Tanh)
+            nc.vector.tensor_tensor(larger[:], dealt(bank), b_sb[rb, jb][:], ALU.max)
+            parts[rb, jb] = (larger, bent)
+
+        def turn_and_scale(rb, jb):
+            larger, bent = parts[rb, jb]
+            bank = psum_x.tile([P, PACK, P], F32, name="turned")
+            for t in range(PACK):
+                nc.tensor.matmul(bank[:, t, :], lhsT=bent[:, t, :], rhs=ident[:], is_transpose=True, start=True, stop=False)
+                nc.tensor.matmul(bank[:, t, :], lhsT=larger[:, t, :], rhs=ident[:], is_transpose=True, start=False, stop=True)
+            nc.vector.tensor_tensor(
+                h_bf[rb][:, jb * P : (jb + 1) * P, :],
+                bank[:].rearrange("p t j -> p j t"),
+                gain_sb[:, rb : rb + 1, :].broadcast_to([P, P, PACK]),
+                ALU.mult,
+            )
+
+        def quantize_h(rb, j0, j1):
+            nc.vector.quantize_mx(
+                out=h_w[rb][:, j0:j1].bitcast(FP8X4), scales=h_s[rb][:, j0:j1],
+                in_=h_bf[rb][:, j0:j1, :].rearrange("p j t -> p (j t)"),
+            )
+
+        def features(units):
+            for n, (rb, jb) in enumerate(units):
+                first_features(rb, jb)
+                if n > 0:
+                    turn_and_scale(*units[n - 1])
+            turn_and_scale(*units[-1])
+
+        width = S // GROUPS
+
+        def plans_times(words, scales, mb, js):
+            ms = slice(mb * P, (mb + 1) * P)
+            bank = psum_de.tile([P, width], F32, name="de")
+            for a in range(PASSES):
+                nc.tensor.matmul_mx(
+                    out=bank[:],
+                    lhsT=v2_w[a][:, ms].bitcast(FP8X4), lhsT_scale=v2_s[V2_ROW + 4 * a :, ms],
+                    rhs=words[a][:, js].bitcast(FP8X4), rhs_scale=scales[a][:, js],
+                    start=(a == 0), stop=(a == PASSES - 1),
+                )
+            return bank
+
+        def scores(g):
+            js = slice(g * width, (g + 1) * width)
+            score = {}
+            for mb in range(MB):
+                direct = plans_times(v_w, v_s, mb, js)
+                bent_d = kept([P, width], F32, f"bent_d{g}{mb}")
+                nc.scalar.activation(bent_d[:], direct[:], ACT.Tanh, bias=pv_sb[:, mb : mb + 1])
+                through = plans_times(h_w, h_s, mb, js)
+                score[mb] = kept([P, width], F32, f"score{g}{mb}")
+                nc.vector.tensor_tensor(score[mb][:], through[:], bent_d[:], ALU.add)
+                if mb > 0:
+                    put(g, mb - 1, score[mb - 1])
+            put(g, MB - 1, score[MB - 1])
+
+        def put(g, mb, score):
+            js = slice(g * width, (g + 1) * width)
+            places = list3[:, g * width // 16 : (g + 1) * width // 16]
+            nc.vector.tensor_tensor(page[mb][:].indirect(places), score[:], wgo_sb[:, js], ALU.mult)
+            if g == GROUPS - 1:
+                nc.sync.dma_start(out[mb * P : (mb + 1) * P, :], page[mb][:])
+
+        for rb in range(RB):
+            for jb in range(JB):
+                second_features(rb, jb)
+        for rb in range(RB):
+            for a in range(PASSES):
+                round_w1(rb, a)
+                quantize_w1(rb, a)
+        nc.vector.tensor_copy(v2_s[:], tab2_s[:].indirect(list2[:]))
+        for a in range(PASSES):
+            nc.vector.tensor_copy(v2_w[a][:], tab2_w[a][:].indirect(list2[:]))
+        per = JB // GROUPS
+        for g in range(GROUPS):
+            jbs = range(g * per, (g + 1) * per)
+            for rb in range(RB):
+                features([(rb, jb) for jb in jbs])
+                for j0 in range(g * width, (g + 1) * width, 256):
+                    quantize_h(rb, j0, j0 + 256)
+            scores(g)

@@ -25,8 +25,8 @@ RB = H // KP
 JB = S // P
 MB = S2 // P
 V2_ROW = 4
-CAST_COLS = 256
-CAST_ENGINES = "vvvsssss"
+CAST_COLS = 128
+CAST_ENGINES = ""
 GROUPS = 1
 
 
@@ -37,10 +37,10 @@ def tile_list_attempt_page_scores_kernel(
     nc = tc.nc
     with ExitStack() as ctx:
         keep = ctx.enter_context(tc.tile_pool(name="keep", bufs=1))
-        ring = ctx.enter_context(tc.tile_pool(name="ring", bufs=3))
-        psum_ab = ctx.enter_context(tc.psum_pool(name="psum_ab", bufs=3))
+        ring = ctx.enter_context(tc.tile_pool(name="ring", bufs=4))
+        psum_ab = ctx.enter_context(tc.psum_pool(name="psum_ab", bufs=4))
         psum_x = ctx.enter_context(tc.psum_pool(name="psum_x", bufs=2))
-        psum_de = ctx.enter_context(tc.psum_pool(name="psum_de", bufs=3))
+        psum_de = ctx.enter_context(tc.psum_pool(name="psum_de", bufs=2))
 
         def kept(shape, dtype, name):
             return keep.tile(shape, dtype, name=name, align_bytes=64)
@@ -52,7 +52,7 @@ def tile_list_attempt_page_scores_kernel(
         tab2_w = [kept([P, T], U32, f"tab2_w{a}") for a in range(PASSES)]
         tab_s = kept([P, PASSES * T], U8, "tab_s")
         tab2_s = kept([P, T], U8, "tab2_s")
-        w4_w = kept([P, PASSES, 2 * H], U8, "w4_w")
+        w4_w = [kept([P, PASSES, 2 * KP], U8, f"w4_w{rb}") for rb in range(RB)]
         w4_s = kept([P, PASSES * H], U8, "w4_s")
         w1_raw = [[kept([P, PACK, KP], F32, f"w1_raw{rb}{a}") for a in range(PASSES)] for rb in range(RB)]
         gain_sb = kept([P, RB, PACK], F32, "gain_sb")
@@ -71,32 +71,46 @@ def tile_list_attempt_page_scores_kernel(
         def load_words(tile, words):
             nc.sync.dma_start(tile[:].bitcast(I32), words.rearrange("p t i -> p (t i)").bitcast(I32))
 
-        def load_planes(tile, scales):
+        def load_planes(tile, scales, queue):
             for q in range(4):
-                nc.sync.dma_start(
+                queue.dma_start(
                     tile[32 * q : 32 * q + 4, :].bitcast(I32).rearrange("r (a c) -> r a c", a=PASSES),
                     scales[:, 4 * q : 4 * q + 4, :].rearrange("a r c -> r a c").bitcast(I32),
                 )
 
+        def load_w1(rb, a):
+            nc.sync.dma_start(
+                w1_raw[rb][a][:],
+                w1[a * KP : (a + 1) * KP, rb * KP : (rb + 1) * KP].rearrange("(p j) c -> p j c", j=PACK),
+            )
+
+        def load_w4(rb):
+            nc.sync.dma_start(
+                w4_w[rb][:].bitcast(I32),
+                w4_words[:, :, 2 * rb * KP : 2 * (rb + 1) * KP].rearrange("a p c -> p a c").bitcast(I32),
+            )
+
+        def load_rows():
+            nc.scalar.dma_start(rows[0:RB, :], gain.rearrange("(b r) -> b r", b=RB))
+            nc.scalar.dma_start(rows[RB : RB + 1, :], pv.rearrange("(o m) -> o m", o=1))
+
         nc.sync.dma_start(list1[:], offs)
-        nc.sync.dma_start(w4_w[:].bitcast(I32), w4_words.rearrange("a p c -> p a c").bitcast(I32))
-        load_planes(tab_s, tab_scales)
-        for a in range(PASSES):
-            load_words(tab_w[a], tab_words[a])
-        load_planes(w4_s, w4_scales)
-        nc.sync.dma_start(rows[0:RB, :], gain.rearrange("(b r) -> b r", b=RB))
-        nc.sync.dma_start(rows[RB : RB + 1, :], pv.rearrange("(o m) -> o m", o=1))
-        for rb in range(RB):
-            for a in range(PASSES):
-                nc.sync.dma_start(
-                    w1_raw[rb][a][:],
-                    w1[a * KP : (a + 1) * KP, rb * KP : (rb + 1) * KP].rearrange("(p j) c -> p j c", j=PACK),
-                )
+        load_words(tab_w[0], tab_words[0])
+        load_planes(tab_s, tab_scales, nc.sync)
+        load_words(tab_w[1], tab_words[1])
+        load_w4(0)
+        load_planes(w4_s, w4_scales, nc.sync)
         nc.sync.dma_start(list2[:], offs2)
-        nc.sync.dma_start(list3[:], offs3)
+        load_w1(0, 0)
+        load_rows()
+        load_w4(1)
+        load_w1(0, 1)
+        load_w1(1, 0)
+        load_w1(1, 1)
         for a in range(PASSES):
             load_words(tab2_w[a], tab2_words[a])
         nc.sync.dma_start(wgo_sb[:], wgo)
+        nc.sync.dma_start(list3[:], offs3)
         for mb in range(MB):
             nc.sync.dma_start(page[mb][:], page1[mb * P : (mb + 1) * P, :])
 
@@ -105,21 +119,32 @@ def tile_list_attempt_page_scores_kernel(
                 tab2_s[32 * q + V2_ROW : 32 * q + V2_ROW + 4 * PASSES, :].bitcast(I32),
                 tab2_scales[:, 4 * q : 4 * q + 4, :].bitcast(I32),
             )
-        bank = psum_x.tile([P, PACK, P], F32, name="turned")
-        for t in range(PACK):
-            nc.tensor.transpose(bank[:, t, :], rows[:, t::PACK], ident[:])
-        nc.scalar.copy(gain_sb[:], bank[:, :, 0:RB].rearrange("p t b -> p b t"))
-        bank = psum_x.tile([P, PACK, P], F32, name="turned")
-        for mb in range(MB):
-            nc.tensor.transpose(bank[:, mb, :], rows[:, mb * P : (mb + 1) * P], ident[:])
-        nc.scalar.copy(pv_sb[:], bank[:, :, RB])
+
+        def turn_rows():
+            bank = psum_x.tile([P, PACK, P], F32, name="turned")
+            for t in range(PACK):
+                nc.tensor.transpose(bank[:, t, :], rows[:, t::PACK], ident[:])
+            nc.scalar.copy(gain_sb[:], bank[:, :, 0:RB].rearrange("p t b -> p b t"))
+            bank = psum_x.tile([P, PACK, P], F32, name="turned")
+            for mb in range(MB):
+                nc.tensor.transpose(bank[:, mb, :], rows[:, mb * P : (mb + 1) * P], ident[:])
+            nc.scalar.copy(pv_sb[:], bank[:, :, RB])
 
         v_s = [kept([P, S], U8, f"v_s{a}") for a in range(PASSES)]
         v_w = [kept([P, S], U32, f"v_w{a}") for a in range(PASSES)]
-        for a in range(PASSES):
+
+        def pick_v_s(a):
             nc.vector.tensor_copy(v_s[a][:], tab_s[:, a * T : (a + 1) * T].indirect(list1[:]))
-        for a in range(PASSES):
-            nc.vector.tensor_copy(v_w[a][:], tab_w[a][:].indirect(list1[:]))
+
+        def pick_v_w(a, j0=0, j1=S):
+            nc.vector.tensor_copy(v_w[a][:, j0:j1], tab_w[a][:].indirect(list1[:, j0 // 16 : j1 // 16]))
+
+        def pick_v2_s():
+            nc.vector.tensor_copy(v2_s[:], tab2_s[:].indirect(list2[:]))
+
+        def pick_v2_w(a, m0=0, m1=S2):
+            nc.vector.tensor_copy(v2_w[a][:, m0:m1], tab2_w[a][:].indirect(list2[:, m0 // 16 : m1 // 16]))
+
         v2_s = kept([P, S2], U8, "v2_s")
         v2_w = [kept([P, S2], U32, f"v2_w{a}") for a in range(PASSES)]
 
@@ -135,7 +160,7 @@ def tile_list_attempt_page_scores_kernel(
                 nc.tensor.matmul_mx(
                     out=bank[:],
                     lhsT=v_w[a][:, js].bitcast(FP8X4), lhsT_scale=v_s[a][:, js],
-                    rhs=w4_w[:, a, 2 * rb * KP : 2 * (rb + 1) * KP].bitcast(FP4X4),
+                    rhs=w4_w[rb][:, a, :].bitcast(FP4X4),
                     rhs_scale=w4_s[:, a * H + rb * KP : a * H + (rb + 1) * KP],
                     start=(a == 0), stop=(a == PASSES - 1),
                 )
@@ -146,12 +171,11 @@ def tile_list_attempt_page_scores_kernel(
         w1_s = [[kept([P, KP], U8, f"w1_s{rb}{a}") for a in range(PASSES)] for rb in range(RB)]
         w1_bf = [[kept([P, KP, PACK], BF16, f"w1_bf{rb}{a}") for a in range(PASSES)] for rb in range(RB)]
 
-        def round_w1(rb, a):
-            for piece in range(KP // CAST_COLS):
-                cs = slice(piece * CAST_COLS, (piece + 1) * CAST_COLS)
+        def round_w1(rb, a, eng, c0, c1):
+            if True:
+                cs = slice(c0, c1)
                 dst = w1_bf[rb][a][:, cs, :].rearrange("p (c i) j -> p c j i", i=4)
                 src = w1_raw[rb][a][:, :, cs].rearrange("p j (c i) -> p c j i", i=4)
-                eng = CAST_ENGINES[(rb * PASSES + a) * (KP // CAST_COLS) + piece]
                 if eng == "v":
                     nc.vector.tensor_copy(dst, src)
                 elif eng == "g":
@@ -159,16 +183,18 @@ def tile_list_attempt_page_scores_kernel(
                 else:
                     nc.scalar.copy(dst, src)
 
-        def quantize_w1(rb, a):
+        def quantize_w1(rb, a, c0=0, c1=KP):
             nc.vector.quantize_mx(
-                out=w1_w[rb][a][:].bitcast(FP8X4), scales=w1_s[rb][a][:],
-                in_=w1_bf[rb][a][:].rearrange("p c j -> p (c j)"),
+                out=w1_w[rb][a][:, c0:c1].bitcast(FP8X4), scales=w1_s[rb][a][:, c0:c1],
+                in_=w1_bf[rb][a][:, c0:c1, :].rearrange("p c j -> p (c j)"),
             )
 
         h_bf = [kept([P, S, PACK], BF16, f"h_bf{rb}") for rb in range(RB)]
         h_w = [kept([P, S], U32, f"h_w{rb}") for rb in range(RB)]
         h_s = [kept([P, S], U8, f"h_s{rb}") for rb in range(RB)]
         parts = {}
+        banks = {}
+        turned = {}
 
         def first_features(rb, jb):
             js = slice(jb * P, (jb + 1) * P)
@@ -180,18 +206,28 @@ def tile_list_attempt_page_scores_kernel(
                     rhs=w1_w[rb][a][:].bitcast(FP8X4), rhs_scale=w1_s[rb][a][:],
                     start=(a == 0), stop=(a == PASSES - 1),
                 )
-            larger = ring.tile([P, PACK, P], F32, name="larger")
-            bent = ring.tile([P, PACK, P], F32, name="bent")
-            nc.scalar.activation(bent[:], dealt(bank), ACT.Tanh)
-            nc.vector.tensor_tensor(larger[:], dealt(bank), b_sb[rb, jb][:], ALU.max)
-            parts[rb, jb] = (larger, bent)
+            banks[rb, jb] = bank
 
-        def turn_and_scale(rb, jb):
-            larger, bent = parts[rb, jb]
+        def bend(rb, jb):
+            bent = ring.tile([P, PACK, P], F32, name="bent")
+            nc.scalar.activation(bent[:], dealt(banks[rb, jb]), ACT.Tanh)
+            parts[rb, jb, 1] = bent
+
+        def larger_of(rb, jb):
+            larger = ring.tile([P, PACK, P], F32, name="larger")
+            nc.vector.tensor_tensor(larger[:], dealt(banks[rb, jb]), b_sb[rb, jb][:], ALU.max)
+            parts[rb, jb, 0] = larger
+
+        def turn(rb, jb):
+            larger, bent = parts[rb, jb, 0], parts[rb, jb, 1]
             bank = psum_x.tile([P, PACK, P], F32, name="turned")
             for t in range(PACK):
                 nc.tensor.matmul(bank[:, t, :], lhsT=bent[:, t, :], rhs=ident[:], is_transpose=True, start=True, stop=False)
                 nc.tensor.matmul(bank[:, t, :], lhsT=larger[:, t, :], rhs=ident[:], is_transpose=True, start=False, stop=True)
+            turned[rb, jb] = bank
+
+        def scale(rb, jb):
+            bank = turned[rb, jb]
             nc.vector.tensor_tensor(
                 h_bf[rb][:, jb * P : (jb + 1) * P, :],
                 bank[:].rearrange("p t j -> p j t"),
@@ -199,18 +235,21 @@ def tile_list_attempt_page_scores_kernel(
                 ALU.mult,
             )
 
+        def scale_on_scalar(rb, jb):
+            bank = turned[rb, jb]
+            rounded = ring.tile([P, PACK, P], BF16, name="rounded")
+            for t in range(PACK):
+                nc.scalar.activation(rounded[:, t, :], bank[:, t, :], ACT.Copy, scale=gain_sb[:, rb, t : t + 1])
+            nc.scalar.copy(
+                h_bf[rb][:, jb * P : (jb + 1) * P, :].rearrange("p (c i) t -> p c t i", i=4),
+                rounded[:].rearrange("p t (c i) -> p c t i", i=4),
+            )
+
         def quantize_h(rb, j0, j1):
             nc.vector.quantize_mx(
                 out=h_w[rb][:, j0:j1].bitcast(FP8X4), scales=h_s[rb][:, j0:j1],
                 in_=h_bf[rb][:, j0:j1, :].rearrange("p j t -> p (j t)"),
             )
-
-        def features(units):
-            for n, (rb, jb) in enumerate(units):
-                first_features(rb, jb)
-                if n > 0:
-                    turn_and_scale(*units[n - 1])
-            turn_and_scale(*units[-1])
 
         width = S // GROUPS
 
@@ -226,42 +265,116 @@ def tile_list_attempt_page_scores_kernel(
                 )
             return bank
 
-        def scores(g):
-            js = slice(g * width, (g + 1) * width)
-            score = {}
-            for mb in range(MB):
-                direct = plans_times(v_w, v_s, mb, js)
-                bent_d = kept([P, width], F32, f"bent_d{g}{mb}")
-                nc.scalar.activation(bent_d[:], direct[:], ACT.Tanh, bias=pv_sb[:, mb : mb + 1])
-                through = plans_times(h_w, h_s, mb, js)
-                score[mb] = kept([P, width], F32, f"score{g}{mb}")
-                nc.vector.tensor_tensor(score[mb][:], through[:], bent_d[:], ALU.add)
-                if mb > 0:
-                    put(g, mb - 1, score[mb - 1])
-            put(g, MB - 1, score[MB - 1])
+        bent_d = {}
+        score = {}
 
-        def put(g, mb, score):
+        def direct_part(g, mb):
+            js = slice(g * width, (g + 1) * width)
+            direct = plans_times(v_w, v_s, mb, js)
+            bent_d[g, mb] = kept([P, width], F32, f"bent_d{g}{mb}")
+            nc.scalar.activation(bent_d[g, mb][:], direct[:], ACT.Tanh, bias=pv_sb[:, mb : mb + 1])
+
+        def sum_part(g, mb):
+            js = slice(g * width, (g + 1) * width)
+            through = plans_times(h_w, h_s, mb, js)
+            score[g, mb] = kept([P, width], F32, f"score{g}{mb}")
+            nc.vector.tensor_tensor(score[g, mb][:], through[:], bent_d[g, mb][:], ALU.add)
+
+        flipped = {}
+
+        def flip_bent(mb):
+            bank = psum_ab.tile([P, JB, P], F32, name="ab")
+            for jb in range(JB):
+                nc.tensor.transpose(bank[:, jb, :], bent_d[0, mb][:, jb * P : (jb + 1) * P], ident[:])
+            flipped[mb] = kept([P, JB, P], F32, f"flipped{mb}")
+            nc.scalar.copy(flipped[mb][:], bank[:])
+
+        def sum_on_pe(mb):
+            ms = slice(mb * P, (mb + 1) * P)
+            bank = psum_ab.tile([P, JB, P], F32, name="ab")
+            for jb in range(JB):
+                js = slice(jb * P, (jb + 1) * P)
+                for a in range(PASSES):
+                    nc.tensor.matmul_mx(
+                        out=bank[:, jb, :],
+                        lhsT=h_w[a][:, js].bitcast(FP8X4), lhsT_scale=h_s[a][:, js],
+                        rhs=v2_w[a][:, ms].bitcast(FP8X4), rhs_scale=v2_s[V2_ROW + 4 * a :, ms],
+                        start=(a == 0), stop=(a == PASSES - 1),
+                    )
+            through = kept([P, JB, P], F32, f"through{mb}")
+            nc.scalar.copy(through[:], bank[:])
+            bank = psum_x.tile([P, JB, P], F32, name="turned")
+            for jb in range(JB):
+                nc.tensor.matmul(bank[:, jb, :], lhsT=flipped[mb][:, jb, :], rhs=ident[:], is_transpose=True, start=True, stop=False)
+                nc.tensor.matmul(bank[:, jb, :], lhsT=through[:, jb, :], rhs=ident[:], is_transpose=True, start=False, stop=True)
+            score[0, mb] = kept([P, S], F32, f"score{mb}")
+            nc.scalar.copy(score[0, mb][:], bank[:].rearrange("p a b -> p (a b)"))
+
+        def put(g, mb):
             js = slice(g * width, (g + 1) * width)
             places = list3[:, g * width // 16 : (g + 1) * width // 16]
-            nc.vector.tensor_tensor(page[mb][:].indirect(places), score[:], wgo_sb[:, js], ALU.mult)
+            nc.vector.tensor_tensor(page[mb][:].indirect(places), score[g, mb][:], wgo_sb[:, js], ALU.mult)
             if g == GROUPS - 1:
                 nc.sync.dma_start(out[mb * P : (mb + 1) * P, :], page[mb][:])
 
-        for rb in range(RB):
-            for jb in range(JB):
-                second_features(rb, jb)
-        for rb in range(RB):
-            for a in range(PASSES):
-                round_w1(rb, a)
-                quantize_w1(rb, a)
-        nc.vector.tensor_copy(v2_s[:], tab2_s[:].indirect(list2[:]))
-        for a in range(PASSES):
-            nc.vector.tensor_copy(v2_w[a][:], tab2_w[a][:].indirect(list2[:]))
-        per = JB // GROUPS
-        for g in range(GROUPS):
-            jbs = range(g * per, (g + 1) * per)
-            for rb in range(RB):
-                features([(rb, jb) for jb in jbs])
-                for j0 in range(g * width, (g + 1) * width, 256):
-                    quantize_h(rb, j0, j0 + 256)
-            scores(g)
+        pick_v_w(0)
+        pick_v_s(0)
+        pick_v_s(1)
+        pick_v_w(1, 0, 256)
+        pick_v_w(1, 256, 512)
+        pick_v2_s()
+        for jb in range(JB):
+            second_features(0, jb)
+        turn_rows()
+        round_w1(0, 0, "v", 0, 512)
+        quantize_w1(0, 0)
+        round_w1(0, 1, "s", 0, 192)
+        round_w1(0, 1, "v", 192, 512)
+        quantize_w1(0, 1, 256, 512)
+        quantize_w1(0, 1, 0, 256)
+        for jb in range(JB):
+            second_features(1, jb)
+        units = [(rb, jb) for rb in range(RB) for jb in range(JB)]
+        def front(rb, jb):
+            first_features(rb, jb)
+            larger_of(rb, jb)
+            bend(rb, jb)
+        def back(rb, jb):
+            turn(rb, jb)
+            if (rb, jb) in []:
+                scale_on_scalar(rb, jb)
+            else:
+                scale(rb, jb)
+        def run(first, last):
+            for n in range(first, last):
+                front(*units[n])
+                if n > 0:
+                    back(*units[n - 1])
+        run(0, 2)
+        round_w1(1, 0, "s", 0, 256)
+        round_w1(1, 0, "s", 256, 512)
+        quantize_w1(1, 0)
+        run(2, 3)
+        round_w1(1, 1, "s", 0, 192)
+        round_w1(1, 1, "s", 192, 384)
+        round_w1(1, 1, "v", 384, 512)
+        quantize_w1(1, 1)
+        run(3, 6)
+        pick_v2_w(0)
+        quantize_h(0, 0, 512)
+        run(6, 8)
+        pick_v2_w(1)
+        direct_part(0, 0)
+        back(*units[7])
+        quantize_h(1, 0, 256)
+        quantize_h(1, 256, 512)
+        sum_part(0, 0)
+        for mb in range(1, MB):
+            direct_part(0, mb)
+            if mb < 1:
+                sum_part(0, mb)
+            else:
+                flip_bent(mb)
+                sum_on_pe(mb)
+            put(0, mb - 1)
+        put(0, MB - 1)

@@ -52,7 +52,7 @@ def tile_list_attempt_page_scores_kernel(
         tab2_w = [kept([P, T], U32, f"tab2_w{a}") for a in range(PASSES)]
         tab_s = kept([P, PASSES * T], U8, "tab_s")
         tab2_s = kept([P, T], U8, "tab2_s")
-        w4_w = [kept([P, PASSES, 2 * KP], U8, f"w4_w{rb}") for rb in range(RB)]
+        w4_w = kept([P, PASSES, 2 * H], U8, "w4_w")
         w4_s = kept([P, PASSES * H], U8, "w4_s")
         w1_raw = [[kept([P, PACK, KP], F32, f"w1_raw{rb}{a}") for a in range(PASSES)] for rb in range(RB)]
         gain_sb = kept([P, RB, PACK], F32, "gain_sb")
@@ -63,8 +63,8 @@ def tile_list_attempt_page_scores_kernel(
 
         rows = kept([P, KP], F32, "rows")
         make_identity(nc, ident[:])
-        nc.gpsimd.memset(rows[:], 0.0)
         nc.vector.memset(tab_s[:].bitcast(I32), 0)
+        nc.vector.memset(rows[:], 0.0)
         nc.vector.memset(w4_s[:].bitcast(I32), 0)
         nc.vector.memset(tab2_s[:].bitcast(I32), 0)
 
@@ -84,27 +84,31 @@ def tile_list_attempt_page_scores_kernel(
                 w1[a * KP : (a + 1) * KP, rb * KP : (rb + 1) * KP].rearrange("(p j) c -> p j c", j=PACK),
             )
 
-        def load_w4(rb):
-            nc.sync.dma_start(
-                w4_w[rb][:].bitcast(I32),
-                w4_words[:, :, 2 * rb * KP : 2 * (rb + 1) * KP].rearrange("a p c -> p a c").bitcast(I32),
-            )
+        def load_w4():
+            nc.sync.dma_start(w4_w[:].bitcast(I32), w4_words.rearrange("a p c -> p a c").bitcast(I32))
+
+        def load_planes2():
+            for q in range(4):
+                nc.sync.dma_start(
+                    tab2_s[32 * q + V2_ROW : 32 * q + V2_ROW + 4 * PASSES, :].bitcast(I32),
+                    tab2_scales[:, 4 * q : 4 * q + 4, :].bitcast(I32),
+                )
 
         def load_rows():
-            nc.scalar.dma_start(rows[0:RB, :], gain.rearrange("(b r) -> b r", b=RB))
-            nc.scalar.dma_start(rows[RB : RB + 1, :], pv.rearrange("(o m) -> o m", o=1))
+            nc.sync.dma_start(rows[0:RB, :], gain.rearrange("(b r) -> b r", b=RB))
+            nc.sync.dma_start(rows[RB : RB + 1, :], pv.rearrange("(o m) -> o m", o=1))
 
-        nc.sync.dma_start(list1[:], offs)
         load_words(tab_w[0], tab_words[0])
+        nc.sync.dma_start(list1[:], offs)
         load_planes(tab_s, tab_scales, nc.sync)
         load_words(tab_w[1], tab_words[1])
-        load_w4(0)
+        load_w4()
         load_planes(w4_s, w4_scales, nc.sync)
-        nc.sync.dma_start(list2[:], offs2)
         load_w1(0, 0)
-        load_rows()
-        load_w4(1)
+        nc.sync.dma_start(list2[:], offs2)
+        load_planes2()
         load_w1(0, 1)
+        load_rows()
         load_w1(1, 0)
         load_w1(1, 1)
         for a in range(PASSES):
@@ -114,11 +118,6 @@ def tile_list_attempt_page_scores_kernel(
         for mb in range(MB):
             nc.sync.dma_start(page[mb][:], page1[mb * P : (mb + 1) * P, :])
 
-        for q in range(4):
-            nc.gpsimd.dma_start(
-                tab2_s[32 * q + V2_ROW : 32 * q + V2_ROW + 4 * PASSES, :].bitcast(I32),
-                tab2_scales[:, 4 * q : 4 * q + 4, :].bitcast(I32),
-            )
 
         def turn_rows():
             bank = psum_x.tile([P, PACK, P], F32, name="turned")
@@ -160,7 +159,7 @@ def tile_list_attempt_page_scores_kernel(
                 nc.tensor.matmul_mx(
                     out=bank[:],
                     lhsT=v_w[a][:, js].bitcast(FP8X4), lhsT_scale=v_s[a][:, js],
-                    rhs=w4_w[rb][:, a, :].bitcast(FP4X4),
+                    rhs=w4_w[:, a, 2 * rb * KP : 2 * (rb + 1) * KP].bitcast(FP4X4),
                     rhs_scale=w4_s[:, a * H + rb * KP : a * H + (rb + 1) * KP],
                     start=(a == 0), stop=(a == PASSES - 1),
                 )
@@ -251,11 +250,10 @@ def tile_list_attempt_page_scores_kernel(
                 in_=h_bf[rb][:, j0:j1, :].rearrange("p j t -> p (j t)"),
             )
 
-        width = S // GROUPS
-
-        def plans_times(words, scales, mb, js):
+        def plans_times(words, scales, mb, j0, j1):
             ms = slice(mb * P, (mb + 1) * P)
-            bank = psum_de.tile([P, width], F32, name="de")
+            js = slice(j0, j1)
+            bank = psum_de.tile([P, j1 - j0], F32, name="de")
             for a in range(PASSES):
                 nc.tensor.matmul_mx(
                     out=bank[:],
@@ -268,24 +266,22 @@ def tile_list_attempt_page_scores_kernel(
         bent_d = {}
         score = {}
 
-        def direct_part(g, mb):
-            js = slice(g * width, (g + 1) * width)
-            direct = plans_times(v_w, v_s, mb, js)
-            bent_d[g, mb] = kept([P, width], F32, f"bent_d{g}{mb}")
-            nc.scalar.activation(bent_d[g, mb][:], direct[:], ACT.Tanh, bias=pv_sb[:, mb : mb + 1])
+        def direct_part(mb):
+            direct = plans_times(v_w, v_s, mb, 0, S)
+            bent_d[mb] = kept([P, S], F32, f"bent_d{mb}")
+            nc.scalar.activation(bent_d[mb][:], direct[:], ACT.Tanh, bias=pv_sb[:, mb : mb + 1])
 
-        def sum_part(g, mb):
-            js = slice(g * width, (g + 1) * width)
-            through = plans_times(h_w, h_s, mb, js)
-            score[g, mb] = kept([P, width], F32, f"score{g}{mb}")
-            nc.vector.tensor_tensor(score[g, mb][:], through[:], bent_d[g, mb][:], ALU.add)
+        def sum_part(mb, j0, j1):
+            through = plans_times(h_w, h_s, mb, j0, j1)
+            score[mb, j0] = kept([P, j1 - j0], F32, f"score{mb}_{j0}")
+            nc.vector.tensor_tensor(score[mb, j0][:], through[:], bent_d[mb][:, j0:j1], ALU.add)
 
         flipped = {}
 
         def flip_bent(mb):
             bank = psum_ab.tile([P, JB, P], F32, name="ab")
             for jb in range(JB):
-                nc.tensor.transpose(bank[:, jb, :], bent_d[0, mb][:, jb * P : (jb + 1) * P], ident[:])
+                nc.tensor.transpose(bank[:, jb, :], bent_d[mb][:, jb * P : (jb + 1) * P], ident[:])
             flipped[mb] = kept([P, JB, P], F32, f"flipped{mb}")
             nc.scalar.copy(flipped[mb][:], bank[:])
 
@@ -307,14 +303,13 @@ def tile_list_attempt_page_scores_kernel(
             for jb in range(JB):
                 nc.tensor.matmul(bank[:, jb, :], lhsT=flipped[mb][:, jb, :], rhs=ident[:], is_transpose=True, start=True, stop=False)
                 nc.tensor.matmul(bank[:, jb, :], lhsT=through[:, jb, :], rhs=ident[:], is_transpose=True, start=False, stop=True)
-            score[0, mb] = kept([P, S], F32, f"score{mb}")
-            nc.scalar.copy(score[0, mb][:], bank[:].rearrange("p a b -> p (a b)"))
+            score[mb, 0] = kept([P, S], F32, f"score{mb}")
+            nc.scalar.copy(score[mb, 0][:], bank[:].rearrange("p a b -> p (a b)"))
 
-        def put(g, mb):
-            js = slice(g * width, (g + 1) * width)
-            places = list3[:, g * width // 16 : (g + 1) * width // 16]
-            nc.vector.tensor_tensor(page[mb][:].indirect(places), score[g, mb][:], wgo_sb[:, js], ALU.mult)
-            if g == GROUPS - 1:
+        def put(mb, j0, j1):
+            places = list3[:, j0 // 16 : j1 // 16]
+            nc.vector.tensor_tensor(page[mb][:].indirect(places), score[mb, j0][:], wgo_sb[:, j0:j1], ALU.mult)
+            if j1 == S:
                 nc.sync.dma_start(out[mb * P : (mb + 1) * P, :], page[mb][:])
 
         pick_v_w(0)
@@ -322,12 +317,11 @@ def tile_list_attempt_page_scores_kernel(
         pick_v_s(1)
         pick_v_w(1, 0, 256)
         pick_v_w(1, 256, 512)
-        pick_v2_s()
         for jb in range(JB):
             second_features(0, jb)
-        turn_rows()
         round_w1(0, 0, "v", 0, 512)
         quantize_w1(0, 0)
+        pick_v2_s()
         round_w1(0, 1, "s", 0, 192)
         round_w1(0, 1, "v", 192, 512)
         quantize_w1(0, 1, 256, 512)
@@ -339,15 +333,18 @@ def tile_list_attempt_page_scores_kernel(
             first_features(rb, jb)
             larger_of(rb, jb)
             bend(rb, jb)
+
         def back(rb, jb):
             turn(rb, jb)
-            if (rb, jb) in []:
+            if (rb, jb) in [(0, 3)]:
                 scale_on_scalar(rb, jb)
             else:
                 scale(rb, jb)
         def run(first, last):
             for n in range(first, last):
                 front(*units[n])
+                if n == 1:
+                    turn_rows()
                 if n > 0:
                     back(*units[n - 1])
         run(0, 2)
@@ -362,19 +359,23 @@ def tile_list_attempt_page_scores_kernel(
         run(3, 6)
         pick_v2_w(0)
         quantize_h(0, 0, 512)
-        run(6, 8)
-        pick_v2_w(1)
-        direct_part(0, 0)
-        back(*units[7])
+        run(6, 7)
         quantize_h(1, 0, 256)
+        pick_v2_w(1)
+        run(7, 8)
+        direct_part(0)
+        back(*units[7])
         quantize_h(1, 256, 512)
-        sum_part(0, 0)
+        sum_part(0, 0, 256)
+        direct_part(1)
+        flip_bent(1)
+        sum_part(0, 256, 512)
+        sum_on_pe(1)
+        put(0, 0, 256)
+        put(0, 256, 512)
+        for mb in range(2, MB):
+            direct_part(mb)
+            flip_bent(mb)
+            sum_on_pe(mb)
         for mb in range(1, MB):
-            direct_part(0, mb)
-            if mb < 1:
-                sum_part(0, mb)
-            else:
-                flip_bent(mb)
-                sum_on_pe(mb)
-            put(0, mb - 1)
-        put(0, MB - 1)
+            put(mb, 0, S)

@@ -26,8 +26,8 @@ JB = S // P
 MB = S2 // P
 V2_ROW = 4
 CAST_COLS = 128
-CAST_ENGINES = ""
-GROUPS = 1
+CAST_ENGINES = 1
+HOLD = ["b_sb03","b_sb10"]
 
 
 def tile_list_attempt_page_scores_kernel(
@@ -38,9 +38,9 @@ def tile_list_attempt_page_scores_kernel(
     with ExitStack() as ctx:
         keep = ctx.enter_context(tc.tile_pool(name="keep", bufs=1))
         ring = ctx.enter_context(tc.tile_pool(name="ring", bufs=4))
-        psum_ab = ctx.enter_context(tc.psum_pool(name="psum_ab", bufs=4))
+        psum_ab = ctx.enter_context(tc.psum_pool(name="psum_ab", bufs=3))
         psum_x = ctx.enter_context(tc.psum_pool(name="psum_x", bufs=2))
-        psum_de = ctx.enter_context(tc.psum_pool(name="psum_de", bufs=2))
+        psum_de = ctx.enter_context(tc.psum_pool(name="psum_de", bufs=3))
 
         def kept(shape, dtype, name):
             return keep.tile(shape, dtype, name=name, align_bytes=64)
@@ -55,27 +55,26 @@ def tile_list_attempt_page_scores_kernel(
         w4_w = kept([P, PASSES, 2 * H], U8, "w4_w")
         w4_s = kept([P, PASSES * H], U8, "w4_s")
         w1_raw = [[kept([P, PACK, KP], F32, f"w1_raw{rb}{a}") for a in range(PASSES)] for rb in range(RB)]
-        gain_sb = kept([P, RB, PACK], F32, "gain_sb")
+        gain_sb = kept([P, RB, 2 * PACK], F32, "gain_sb")
         pv_sb = kept([P, MB], F32, "pv_sb")
         wgo_sb = kept([P, S], F32, "wgo_sb")
         page = [kept([P, T2], F32, f"page{mb}") for mb in range(MB)]
         ident = kept([P, P], F32, "ident")
 
-        rows = kept([P, KP], F32, "rows")
-        make_identity(nc, ident[:])
+        rows = kept([P, P], F32, "rows")
         nc.vector.memset(tab_s[:].bitcast(I32), 0)
-        nc.vector.memset(rows[:], 0.0)
-        nc.vector.memset(w4_s[:].bitcast(I32), 0)
         nc.vector.memset(tab2_s[:].bitcast(I32), 0)
+        nc.vector.memset(w4_s[:].bitcast(I32), 0)
+        nc.vector.memset(rows[:], 0.0)
 
         def load_words(tile, words):
             nc.sync.dma_start(tile[:].bitcast(I32), words.rearrange("p t i -> p (t i)").bitcast(I32))
 
         def load_planes(tile, scales, queue):
-            for q in range(4):
+            for r in range(4):
                 queue.dma_start(
-                    tile[32 * q : 32 * q + 4, :].bitcast(I32).rearrange("r (a c) -> r a c", a=PASSES),
-                    scales[:, 4 * q : 4 * q + 4, :].rearrange("a r c -> r a c").bitcast(I32),
+                    tile[r::32, :].bitcast(I32).rearrange("q (a c) -> q a c", a=PASSES),
+                    scales[:, r::4, :].rearrange("a q c -> q a c").bitcast(I32),
                 )
 
         def load_w1(rb, a):
@@ -87,30 +86,34 @@ def tile_list_attempt_page_scores_kernel(
         def load_w4():
             nc.sync.dma_start(w4_w[:].bitcast(I32), w4_words.rearrange("a p c -> p a c").bitcast(I32))
 
-        def load_planes2():
-            for q in range(4):
-                nc.sync.dma_start(
+        def load_planes2(queue):
+            for q in (0, 2, 1, 3):
+                queue.dma_start(
                     tab2_s[32 * q + V2_ROW : 32 * q + V2_ROW + 4 * PASSES, :].bitcast(I32),
                     tab2_scales[:, 4 * q : 4 * q + 4, :].bitcast(I32),
                 )
 
-        def load_rows():
-            nc.sync.dma_start(rows[0:RB, :], gain.rearrange("(b r) -> b r", b=RB))
-            nc.sync.dma_start(rows[RB : RB + 1, :], pv.rearrange("(o m) -> o m", o=1))
+        def load_gain():
+            nc.sync.dma_start(gain_sb[:, :, 0:PACK], gain.rearrange("(b p t) -> p b t", p=P, t=PACK))
+
+        def load_pv():
+            nc.sync.dma_start(rows[0:MB, :], pv.rearrange("(b p) -> b p", p=P))
 
         load_words(tab_w[0], tab_words[0])
         nc.sync.dma_start(list1[:], offs)
         load_planes(tab_s, tab_scales, nc.sync)
-        load_words(tab_w[1], tab_words[1])
+        nc.sync.dma_start(list2[:], offs2)
         load_w4()
         load_planes(w4_s, w4_scales, nc.sync)
+        load_words(tab_w[1], tab_words[1])
         load_w1(0, 0)
-        nc.sync.dma_start(list2[:], offs2)
-        load_planes2()
         load_w1(0, 1)
-        load_rows()
         load_w1(1, 0)
+        load_gain()
         load_w1(1, 1)
+        load_pv()
+        load_planes2(nc.gpsimd)
+        make_identity(nc, ident[:])
         for a in range(PASSES):
             load_words(tab2_w[a], tab2_words[a])
         nc.sync.dma_start(wgo_sb[:], wgo)
@@ -120,14 +123,9 @@ def tile_list_attempt_page_scores_kernel(
 
 
         def turn_rows():
-            bank = psum_x.tile([P, PACK, P], F32, name="turned")
-            for t in range(PACK):
-                nc.tensor.transpose(bank[:, t, :], rows[:, t::PACK], ident[:])
-            nc.scalar.copy(gain_sb[:], bank[:, :, 0:RB].rearrange("p t b -> p b t"))
-            bank = psum_x.tile([P, PACK, P], F32, name="turned")
-            for mb in range(MB):
-                nc.tensor.transpose(bank[:, mb, :], rows[:, mb * P : (mb + 1) * P], ident[:])
-            nc.scalar.copy(pv_sb[:], bank[:, :, RB])
+            bank = psum_x.tile([P, P], F32, name="turned")
+            nc.tensor.transpose(bank[:], rows[:], ident[:])
+            nc.scalar.copy(pv_sb[:], bank[:, 0:MB])
 
         v_s = [kept([P, S], U8, f"v_s{a}") for a in range(PASSES)]
         v_w = [kept([P, S], U32, f"v_w{a}") for a in range(PASSES)]
@@ -141,20 +139,26 @@ def tile_list_attempt_page_scores_kernel(
         def pick_v2_s():
             nc.vector.tensor_copy(v2_s[:], tab2_s[:].indirect(list2[:]))
 
-        def pick_v2_w(a, m0=0, m1=S2):
-            nc.vector.tensor_copy(v2_w[a][:, m0:m1], tab2_w[a][:].indirect(list2[:, m0 // 16 : m1 // 16]))
+        def pick_v2_w(a):
+            v2_w[a] = keep.tile([P, S2], U32, name=f"v2_w{a}", tag=HOLD[a], align_bytes=64)
+            nc.vector.tensor_copy(v2_w[a][:], tab2_w[a][:].indirect(list2[:]))
 
         v2_s = kept([P, S2], U8, "v2_s")
-        v2_w = [kept([P, S2], U32, f"v2_w{a}") for a in range(PASSES)]
+        v2_w = {}
 
         def dealt(bank):
             return bank[:].rearrange("p (m t) -> p t m", t=PACK)
 
         b_sb = {}
 
-        def second_features(rb, jb):
+        def second_features(rb, jb, late=False):
             js = slice(jb * P, (jb + 1) * P)
-            bank = psum_ab.tile([P, KP], F32, name="ab")
+            if late:
+                bank = psum_ab.tile([P, KP], F32, name="ab")
+            elif jb % 2:
+                bank = psum_de.tile([P, KP], F32, name="de")
+            else:
+                bank = psum_x.tile([P, KP], F32, name="turned")
             for a in range(PASSES):
                 nc.tensor.matmul_mx(
                     out=bank[:],
@@ -168,9 +172,11 @@ def tile_list_attempt_page_scores_kernel(
 
         w1_w = [[kept([P, KP], U32, f"w1_w{rb}{a}") for a in range(PASSES)] for rb in range(RB)]
         w1_s = [[kept([P, KP], U8, f"w1_s{rb}{a}") for a in range(PASSES)] for rb in range(RB)]
-        w1_bf = [[kept([P, KP, PACK], BF16, f"w1_bf{rb}{a}") for a in range(PASSES)] for rb in range(RB)]
+        w1_bf = [{} for rb in range(RB)]
 
         def round_w1(rb, a, eng, c0, c1):
+            if a not in w1_bf[rb]:
+                w1_bf[rb][a] = keep.tile([P, KP, PACK], BF16, name=f"w1_bf{rb}{a}", tag=f"w1_bf{CAST_ENGINES * rb + a}", align_bytes=64)
             if True:
                 cs = slice(c0, c1)
                 dst = w1_bf[rb][a][:, cs, :].rearrange("p (c i) j -> p c j i", i=4)
@@ -178,7 +184,9 @@ def tile_list_attempt_page_scores_kernel(
                 if eng == "v":
                     nc.vector.tensor_copy(dst, src)
                 elif eng == "g":
-                    nc.gpsimd.tensor_copy(dst, src)
+                    nc.gpsimd.tensor_scalar(
+                        w1_bf[rb][a][:, cs, :], w1_raw[rb][a][:, :, cs].rearrange("p j c -> p c j"), 1.0, 0.0, ALU.mult, ALU.add
+                    )
                 else:
                     nc.scalar.copy(dst, src)
 
@@ -230,7 +238,7 @@ def tile_list_attempt_page_scores_kernel(
             nc.vector.tensor_tensor(
                 h_bf[rb][:, jb * P : (jb + 1) * P, :],
                 bank[:].rearrange("p t j -> p j t"),
-                gain_sb[:, rb : rb + 1, :].broadcast_to([P, P, PACK]),
+                gain_sb[:, rb : rb + 1, 0:PACK].broadcast_to([P, P, PACK]),
                 ALU.mult,
             )
 
@@ -317,65 +325,70 @@ def tile_list_attempt_page_scores_kernel(
         pick_v_s(1)
         pick_v_w(1, 0, 256)
         pick_v_w(1, 256, 512)
+        pick_v2_s()
         for jb in range(JB):
             second_features(0, jb)
         round_w1(0, 0, "v", 0, 512)
         quantize_w1(0, 0)
-        pick_v2_s()
-        round_w1(0, 1, "s", 0, 192)
-        round_w1(0, 1, "v", 192, 512)
-        quantize_w1(0, 1, 256, 512)
-        quantize_w1(0, 1, 0, 256)
-        for jb in range(JB):
+        for jb in range(4):
             second_features(1, jb)
+        round_w1(0, 1, "v", 0, 512)
+        quantize_w1(0, 1)
         units = [(rb, jb) for rb in range(RB) for jb in range(JB)]
         def front(rb, jb):
             first_features(rb, jb)
             larger_of(rb, jb)
             bend(rb, jb)
-
+            if rb == 0 and jb >= 4:
+                second_features(1, jb, True)
         def back(rb, jb):
             turn(rb, jb)
-            if (rb, jb) in [(0, 3)]:
+            if (rb, jb) in []:
                 scale_on_scalar(rb, jb)
             else:
                 scale(rb, jb)
         def run(first, last):
             for n in range(first, last):
                 front(*units[n])
-                if n == 1:
-                    turn_rows()
                 if n > 0:
                     back(*units[n - 1])
         run(0, 2)
-        round_w1(1, 0, "s", 0, 256)
-        round_w1(1, 0, "s", 256, 512)
+        round_w1(1, 0, "s", 0, 128)
+        round_w1(1, 0, "s", 128, 256)
+        round_w1(1, 0, "v", 256, 512)
         quantize_w1(1, 0)
         run(2, 3)
-        round_w1(1, 1, "s", 0, 192)
-        round_w1(1, 1, "s", 192, 384)
-        round_w1(1, 1, "v", 384, 512)
+        round_w1(1, 1, "s", 0, 128)
+        round_w1(1, 1, "s", 128, 256)
+        round_w1(1, 1, "s", 256, 384)
+        round_w1(1, 1, "s", 384, 512)
         quantize_w1(1, 1)
-        run(3, 6)
+        run(3, 5)
         pick_v2_w(0)
+        run(5, 6)
+        pick_v2_w(1)
+        turn_rows()
         quantize_h(0, 0, 512)
         run(6, 7)
         quantize_h(1, 0, 256)
-        pick_v2_w(1)
-        run(7, 8)
         direct_part(0)
+        run(7, 8)
+        direct_part(1)
         back(*units[7])
         quantize_h(1, 256, 512)
         sum_part(0, 0, 256)
-        direct_part(1)
-        flip_bent(1)
         sum_part(0, 256, 512)
-        sum_on_pe(1)
+        def summed(mb):
+            if mb < 2:
+                sum_part(mb, 0, S)
+            else:
+                flip_bent(mb)
+                sum_on_pe(mb)
+        summed(1)
         put(0, 0, 256)
         put(0, 256, 512)
         for mb in range(2, MB):
             direct_part(mb)
-            flip_bent(mb)
-            sum_on_pe(mb)
+            summed(mb)
         for mb in range(1, MB):
             put(mb, 0, S)

from contextlib import ExitStack

import concourse.mybir as mybir
from concourse.masks import make_identity

K, H, T, S, S2, T2 = 1024, 1024, 2048, 512, 512, 1024
FLOPS = 2 * (2 * K * H * S + H * S2 * S + K * S2 * S)

F32 = mybir.dt.float32
BF16 = mybir.dt.bfloat16
I32 = mybir.dt.int32
U32 = mybir.dt.uint32
U16 = mybir.dt.uint16
U8 = mybir.dt.uint8
FP8X4 = mybir.dt.float8_e4m3fn_x4
FP4X4 = mybir.dt.float4_e2m1fn_x4
ALU = mybir.AluOpType
ACT = mybir.ActivationFunctionType

P = 128
PACK = 4
KP = P * PACK
PASSES = K // KP
RB = H // KP
JB = S // P
MB = S2 // P
V2_ROW = 4
CAST_COLS = 128
CAST_ENGINES = 1
HOLD = ["b_sb03","b_sb10"]


def tile_list_attempt_page_scores_kernel(
    tc, tab_words, tab_scales, offs, tab2_words, tab2_scales, offs2, offs3,
    w1, w4_words, w4_scales, gain, pv, page1, wgo, out,
):
    nc = tc.nc
    with ExitStack() as ctx:
        keep = ctx.enter_context(tc.tile_pool(name="keep", bufs=1))
        ring = ctx.enter_context(tc.tile_pool(name="ring", bufs=4))
        psum_ab = ctx.enter_context(tc.psum_pool(name="psum_ab", bufs=3))
        psum_x = ctx.enter_context(tc.psum_pool(name="psum_x", bufs=2))
        psum_de = ctx.enter_context(tc.psum_pool(name="psum_de", bufs=3))

        def kept(shape, dtype, name):
            return keep.tile(shape, dtype, name=name, align_bytes=64)

        list1 = kept([P, S // 16], U16, "list1")
        list2 = kept([P, S2 // 16], U16, "list2")
        list3 = kept([P, S // 16], U16, "list3")
        tab_w = [kept([P, T], U32, f"tab_w{a}") for a in range(PASSES)]
        tab2_w = [kept([P, T], U32, f"tab2_w{a}") for a in range(PASSES)]
        tab_s = kept([P, PASSES * T], U8, "tab_s")
        tab2_s = kept([P, T], U8, "tab2_s")
        w4_w = kept([P, PASSES, 2 * H], U8, "w4_w")
        w4_s = kept([P, PASSES * H], U8, "w4_s")
        w1_raw = [[kept([P, PACK, KP], F32, f"w1_raw{rb}{a}") for a in range(PASSES)] for rb in range(RB)]
        gain_sb = kept([P, RB, 2 * PACK], F32, "gain_sb")
        pv_sb = kept([P, MB], F32, "pv_sb")
        wgo_sb = kept([P, S], F32, "wgo_sb")
        page = [kept([P, T2], F32, f"page{mb}") for mb in range(MB)]
        ident = kept([P, P], F32, "ident")

        rows = kept([P, P], F32, "rows")
        nc.vector.memset(tab_s[:].bitcast(I32), 0)
        nc.vector.memset(tab2_s[:].bitcast(I32), 0)
        nc.vector.memset(w4_s[:].bitcast(I32), 0)
        nc.vector.memset(rows[:], 0.0)

        def load_words(tile, words):
            nc.sync.dma_start(tile[:].bitcast(I32), words.rearrange("p t i -> p (t i)").bitcast(I32))

        def load_planes(tile, scales, queue):
            for r in range(4):
                queue.dma_start(
                    tile[r::32, :].bitcast(I32).rearrange("q (a c) -> q a c", a=PASSES),
                    scales[:, r::4, :].rearrange("a q c -> q a c").bitcast(I32),
                )

        def load_w1(rb, a):
            nc.sync.dma_start(
                w1_raw[rb][a][:],
                w1[a * KP : (a + 1) * KP, rb * KP : (rb + 1) * KP].rearrange("(p j) c -> p j c", j=PACK),
            )

        def load_w4():
            nc.sync.dma_start(w4_w[:].bitcast(I32), w4_words.rearrange("a p c -> p a c").bitcast(I32))

        def load_planes2(queue):
            for q in (0, 2, 1, 3):
                queue.dma_start(
                    tab2_s[32 * q + V2_ROW : 32 * q + V2_ROW + 4 * PASSES, :].bitcast(I32),
                    tab2_scales[:, 4 * q : 4 * q + 4, :].bitcast(I32),
                )

        def load_gain():
            nc.sync.dma_start(gain_sb[:, :, 0:PACK], gain.rearrange("(b p t) -> p b t", p=P, t=PACK))

        def load_pv():
            nc.sync.dma_start(rows[0:MB, :], pv.rearrange("(b p) -> b p", p=P))

        load_words(tab_w[0], tab_words[0])
        nc.sync.dma_start(list1[:], offs)
        load_planes(tab_s, tab_scales, nc.sync)
        nc.sync.dma_start(list2[:], offs2)
        load_w4()
        load_planes(w4_s, w4_scales, nc.sync)
        load_words(tab_w[1], tab_words[1])
        load_w1(0, 0)
        load_w1(0, 1)
        load_w1(1, 0)
        load_gain()
        load_w1(1, 1)
        load_pv()
        load_planes2(nc.gpsimd)
        make_identity(nc, ident[:])
        for a in range(PASSES):
            load_words(tab2_w[a], tab2_words[a])
        nc.sync.dma_start(wgo_sb[:], wgo)
        nc.sync.dma_start(list3[:], offs3)
        for mb in range(MB):
            nc.sync.dma_start(page[mb][:], page1[mb * P : (mb + 1) * P, :])


        def turn_rows():
            bank = psum_x.tile([P, P], F32, name="turned")
            nc.tensor.transpose(bank[:], rows[:], ident[:])
            nc.scalar.copy(pv_sb[:], bank[:, 0:MB])

        v_s = [kept([P, S], U8, f"v_s{a}") for a in range(PASSES)]
        v_w = [kept([P, S], U32, f"v_w{a}") for a in range(PASSES)]

        def pick_v_s(a):
            nc.vector.tensor_copy(v_s[a][:], tab_s[:, a * T : (a + 1) * T].indirect(list1[:]))

        def pick_v_w(a, j0=0, j1=S):
            nc.vector.tensor_copy(v_w[a][:, j0:j1], tab_w[a][:].indirect(list1[:, j0 // 16 : j1 // 16]))

        def pick_v2_s():
            nc.vector.tensor_copy(v2_s[:], tab2_s[:].indirect(list2[:]))

        def pick_v2_w(a):
            v2_w[a] = keep.tile([P, S2], U32, name=f"v2_w{a}", tag=HOLD[a], align_bytes=64)
            nc.vector.tensor_copy(v2_w[a][:], tab2_w[a][:].indirect(list2[:]))

        v2_s = kept([P, S2], U8, "v2_s")
        v2_w = {}

        def dealt(bank):
            return bank[:].rearrange("p (m t) -> p t m", t=PACK)

        b_sb = {}

        def second_features(rb, jb, late=False):
            js = slice(jb * P, (jb + 1) * P)
            if late:
                bank = psum_ab.tile([P, KP], F32, name="ab")
            elif jb % 2:
                bank = psum_de.tile([P, KP], F32, name="de")
            else:
                bank = psum_x.tile([P, KP], F32, name="turned")
            for a in range(PASSES):
                nc.tensor.matmul_mx(
                    out=bank[:],
                    lhsT=v_w[a][:, js].bitcast(FP8X4), lhsT_scale=v_s[a][:, js],
                    rhs=w4_w[:, a, 2 * rb * KP : 2 * (rb + 1) * KP].bitcast(FP4X4),
                    rhs_scale=w4_s[:, a * H + rb * KP : a * H + (rb + 1) * KP],
                    start=(a == 0), stop=(a == PASSES - 1),
                )
            b_sb[rb, jb] = kept([P, PACK, P], F32, f"b_sb{rb}{jb}")
            nc.scalar.copy(b_sb[rb, jb][:], dealt(bank))

        w1_w = [[kept([P, KP], U32, f"w1_w{rb}{a}") for a in range(PASSES)] for rb in range(RB)]
        w1_s = [[kept([P, KP], U8, f"w1_s{rb}{a}") for a in range(PASSES)] for rb in range(RB)]
        w1_bf = [{} for rb in range(RB)]

        def round_w1(rb, a, eng, c0, c1):
            if a not in w1_bf[rb]:
                w1_bf[rb][a] = keep.tile([P, KP, PACK], BF16, name=f"w1_bf{rb}{a}", tag=f"w1_bf{CAST_ENGINES * rb + a}", align_bytes=64)
            if True:
                cs = slice(c0, c1)
                dst = w1_bf[rb][a][:, cs, :].rearrange("p (c i) j -> p c j i", i=4)
                src = w1_raw[rb][a][:, :, cs].rearrange("p j (c i) -> p c j i", i=4)
                if eng == "v":
                    nc.vector.tensor_copy(dst, src)
                elif eng == "g":
                    nc.gpsimd.tensor_scalar(
                        w1_bf[rb][a][:, cs, :], w1_raw[rb][a][:, :, cs].rearrange("p j c -> p c j"), 1.0, 0.0, ALU.mult, ALU.add
                    )
                else:
                    nc.scalar.copy(dst, src)

        def quantize_w1(rb, a, c0=0, c1=KP):
            nc.vector.quantize_mx(
                out=w1_w[rb][a][:, c0:c1].bitcast(FP8X4), scales=w1_s[rb][a][:, c0:c1],
                in_=w1_bf[rb][a][:, c0:c1, :].rearrange("p c j -> p (c j)"),
            )

        h_bf = [kept([P, S, PACK], BF16, f"h_bf{rb}") for rb in range(RB)]
        h_w = [kept([P, S], U32, f"h_w{rb}") for rb in range(RB)]
        h_s = [kept([P, S], U8, f"h_s{rb}") for rb in range(RB)]
        parts = {}
        banks = {}
        turned = {}

        def first_features(rb, jb):
            js = slice(jb * P, (jb + 1) * P)
            bank = psum_ab.tile([P, KP], F32, name="ab")
            for a in range(PASSES):
                nc.tensor.matmul_mx(
                    out=bank[:],
                    lhsT=v_w[a][:, js].bitcast(FP8X4), lhsT_scale=v_s[a][:, js],
                    rhs=w1_w[rb][a][:].bitcast(FP8X4), rhs_scale=w1_s[rb][a][:],
                    start=(a == 0), stop=(a == PASSES - 1),
                )
            banks[rb, jb] = bank

        def bend(rb, jb):
            bent = ring.tile([P, PACK, P], F32, name="bent")
            nc.scalar.activation(bent[:], dealt(banks[rb, jb]), ACT.Tanh)
            parts[rb, jb, 1] = bent

        def larger_of(rb, jb):
            larger = ring.tile([P, PACK, P], F32, name="larger")
            nc.vector.tensor_tensor(larger[:], dealt(banks[rb, jb]), b_sb[rb, jb][:], ALU.max)
            parts[rb, jb, 0] = larger

        def turn(rb, jb):
            larger, bent = parts[rb, jb, 0], parts[rb, jb, 1]
            bank = psum_x.tile([P, PACK, P], F32, name="turned")
            for t in range(PACK):
                nc.tensor.matmul(bank[:, t, :], lhsT=bent[:, t, :], rhs=ident[:], is_transpose=True, start=True, stop=False)
                nc.tensor.matmul(bank[:, t, :], lhsT=larger[:, t, :], rhs=ident[:], is_transpose=True, start=False, stop=True)
            turned[rb, jb] = bank

        def scale(rb, jb):
            bank = turned[rb, jb]
            nc.vector.tensor_tensor(
                h_bf[rb][:, jb * P : (jb + 1) * P, :],
                bank[:].rearrange("p t j -> p j t"),
                gain_sb[:, rb : rb + 1, 0:PACK].broadcast_to([P, P, PACK]),
                ALU.mult,
            )

        def scale_on_scalar(rb, jb):
            bank = turned[rb, jb]
            rounded = ring.tile([P, PACK, P], BF16, name="rounded")
            for t in range(PACK):
                nc.scalar.activation(rounded[:, t, :], bank[:, t, :], ACT.Copy, scale=gain_sb[:, rb, t : t + 1])
            nc.scalar.copy(
                h_bf[rb][:, jb * P : (jb + 1) * P, :].rearrange("p (c i) t -> p c t i", i=4),
                rounded[:].rearrange("p t (c i) -> p c t i", i=4),
            )

        def quantize_h(rb, j0, j1):
            nc.vector.quantize_mx(
                out=h_w[rb][:, j0:j1].bitcast(FP8X4), scales=h_s[rb][:, j0:j1],
                in_=h_bf[rb][:, j0:j1, :].rearrange("p j t -> p (j t)"),
            )

        def plans_times(words, scales, mb, j0, j1):
            ms = slice(mb * P, (mb + 1) * P)
            js = slice(j0, j1)
            bank = psum_de.tile([P, j1 - j0], F32, name="de")
            for a in range(PASSES):
                nc.tensor.matmul_mx(
                    out=bank[:],
                    lhsT=v2_w[a][:, ms].bitcast(FP8X4), lhsT_scale=v2_s[V2_ROW + 4 * a :, ms],
                    rhs=words[a][:, js].bitcast(FP8X4), rhs_scale=scales[a][:, js],
                    start=(a == 0), stop=(a == PASSES - 1),
                )
            return bank

        bent_d = {}
        score = {}

        def direct_part(mb):
            direct = plans_times(v_w, v_s, mb, 0, S)
            bent_d[mb] = kept([P, S], F32, f"bent_d{mb}")
            nc.scalar.activation(bent_d[mb][:], direct[:], ACT.Tanh, bias=pv_sb[:, mb : mb + 1])

        def sum_part(mb, j0, j1):
            through = plans_times(h_w, h_s, mb, j0, j1)
            score[mb, j0] = kept([P, j1 - j0], F32, f"score{mb}_{j0}")
            nc.vector.tensor_tensor(score[mb, j0][:], through[:], bent_d[mb][:, j0:j1], ALU.add)

        flipped = {}

        def flip_bent(mb):
            bank = psum_ab.tile([P, JB, P], F32, name="ab")
            for jb in range(JB):
                nc.tensor.transpose(bank[:, jb, :], bent_d[mb][:, jb * P : (jb + 1) * P], ident[:])
            flipped[mb] = kept([P, JB, P], F32, f"flipped{mb}")
            nc.scalar.copy(flipped[mb][:], bank[:])

        def sum_on_pe(mb):
            ms = slice(mb * P, (mb + 1) * P)
            bank = psum_ab.tile([P, JB, P], F32, name="ab")
            for jb in range(JB):
                js = slice(jb * P, (jb + 1) * P)
                for a in range(PASSES):
                    nc.tensor.matmul_mx(
                        out=bank[:, jb, :],
                        lhsT=h_w[a][:, js].bitcast(FP8X4), lhsT_scale=h_s[a][:, js],
                        rhs=v2_w[a][:, ms].bitcast(FP8X4), rhs_scale=v2_s[V2_ROW + 4 * a :, ms],
                        start=(a == 0), stop=(a == PASSES - 1),
                    )
            through = kept([P, JB, P], F32, f"through{mb}")
            nc.scalar.copy(through[:], bank[:])
            bank = psum_x.tile([P, JB, P], F32, name="turned")
            for jb in range(JB):
                nc.tensor.matmul(bank[:, jb, :], lhsT=flipped[mb][:, jb, :], rhs=ident[:], is_transpose=True, start=True, stop=False)
                nc.tensor.matmul(bank[:, jb, :], lhsT=through[:, jb, :], rhs=ident[:], is_transpose=True, start=False, stop=True)
            score[mb, 0] = kept([P, S], F32, f"score{mb}")
            nc.scalar.copy(score[mb, 0][:], bank[:].rearrange("p a b -> p (a b)"))

        def put(mb, j0, j1):
            places = list3[:, j0 // 16 : j1 // 16]
            nc.vector.tensor_tensor(page[mb][:].indirect(places), score[mb, j0][:], wgo_sb[:, j0:j1], ALU.mult)
            if j1 == S:
                nc.sync.dma_start(out[mb * P : (mb + 1) * P, :], page[mb][:])

        pick_v_w(0)
        pick_v_s(0)
        pick_v_s(1)
        pick_v_w(1, 0, 256)
        pick_v_w(1, 256, 512)
        pick_v2_s()
        for jb in range(JB):
            second_features(0, jb)
        round_w1(0, 0, "v", 0, 512)
        quantize_w1(0, 0)
        for jb in range(4):
            second_features(1, jb)
        round_w1(0, 1, "v", 0, 512)
        quantize_w1(0, 1)
        units = [(rb, jb) for rb in range(RB) for jb in range(JB)]
        def front(rb, jb):
            first_features(rb, jb)
            larger_of(rb, jb)
            bend(rb, jb)
            if rb == 0 and jb >= 4:
                second_features(1, jb, True)
        def back(rb, jb):
            turn(rb, jb)
            if (rb, jb) in []:
                scale_on_scalar(rb, jb)
            else:
                scale(rb, jb)
        def run(first, last):
            for n in range(first, last):
                front(*units[n])
                if n > 0:
                    back(*units[n - 1])
        run(0, 2)
        round_w1(1, 0, "s", 0, 128)
        round_w1(1, 0, "s", 128, 256)
        round_w1(1, 0, "v", 256, 512)
        quantize_w1(1, 0)
        run(2, 3)
        round_w1(1, 1, "s", 0, 128)
        round_w1(1, 1, "s", 128, 256)
        round_w1(1, 1, "s", 256, 384)
        round_w1(1, 1, "s", 384, 512)
        quantize_w1(1, 1)
        run(3, 5)
        pick_v2_w(0)
        run(5, 6)
        pick_v2_w(1)
        turn_rows()
        quantize_h(0, 0, 512)
        run(6, 7)
        quantize_h(1, 0, 256)
        direct_part(0)
        run(7, 8)
        direct_part(1)
        back(*units[7])
        quantize_h(1, 256, 512)
        sum_part(0, 0, 256)
        sum_part(0, 256, 512)
        def summed(mb):
            if mb < 2:
                sum_part(mb, 0, S)
            else:
                flip_bent(mb)
                sum_on_pe(mb)
        summed(1)
        put(0, 0, 256)
        put(0, 256, 512)
        for mb in range(2, MB):
            direct_part(mb)
            summed(mb)
        for mb in range(1, MB):
            put(mb, 0, S)
